import numpy as np
import ml_dtypes


def mxq(x, axis, fmt="e4m3"):
    dtype, down = {"e4m3": (ml_dtypes.float8_e4m3fn, 7), "e5m2": (ml_dtypes.float8_e5m2, 14)}[fmt]
    v = np.moveaxis(np.asarray(x, np.float32).astype(ml_dtypes.bfloat16).astype(np.float64), axis, -1)
    blocks = v.reshape(v.shape[:-1] + (-1, 32))
    amax = np.abs(blocks).max(-1, keepdims=True)
    byte = np.maximum(np.where(amax > 0, np.frexp(amax)[1] - 1 + 127, 0) - down, 1)
    scale = np.exp2(byte - 127.0)
    codes = (blocks / scale).astype(np.float32).astype(dtype).astype(np.float64)
    return np.moveaxis((codes * scale).reshape(v.shape), -1, axis)


WIDE = False


def mx_kscale(k):
    if not WIDE:
        return np.ones(k)
    levels = np.array([10, -10, 5, -5, 0])
    if k % 512:
        return np.exp2(np.random.permutation(np.resize(levels, k // 32))).repeat(32)
    a = np.empty((k // 512, 16))
    for p in range(k // 512):
        a[p, :8] = np.random.permutation(np.resize(levels, 8))
        for g in range(8):
            far = levels[np.abs(levels - a[p, g]) >= 10]
            a[p, g + 8] = far[np.random.randint(len(far))]
    return np.exp2(a.ravel()).repeat(32)


BF16 = ml_dtypes.bfloat16


def bf(x):
    return np.asarray(x, np.float32).astype(BF16)


def f64(x):
    return np.asarray(x).astype(np.float64)


E2M1 = np.array([0.0, 0.5, 1.0, 1.5, 2.0, 3.0, 4.0, 6.0, -0.0, -0.5, -1.0, -1.5, -2.0, -3.0, -4.0, -6.0])


def pack_weight(w, fmt):
    k, n = w.shape
    w = f64(bf(w)).reshape(k // 32, 32, n)
    amax = np.abs(w).max(1)
    if fmt == "e4m3":
        byte = np.frexp(amax)[1] - 1 + 127 - 7
    else:
        mant, ex = np.frexp(amax / 6.0)
        byte = np.where(mant > 0.5, ex, ex - 1) + 127
    byte = np.clip(np.where(amax > 0, byte, 1), 1, 254)
    scaled = (w * np.exp2(127.0 - byte)[:, None, :]).reshape(k, n).astype(np.float32)
    by_word = np.ascontiguousarray(scaled.reshape(k // 512, 128, 4, n).transpose(0, 1, 3, 2))
    if fmt == "e4m3":
        words = by_word.astype(ml_dtypes.float8_e4m3fn).view(np.uint8)
    else:
        c = by_word.astype(ml_dtypes.float4_e2m1fn).view(np.uint8) & 0xF
        words = c[..., 0::2] | (c[..., 1::2] << 4)
    return np.ascontiguousarray(words), np.ascontiguousarray(byte.astype(np.uint8).reshape(k // 512, 16, n))


def unpack_weight(words, scales, fmt):
    g, p, n, _ = words.shape
    if fmt == "e4m3":
        vals = np.ascontiguousarray(words).view(ml_dtypes.float8_e4m3fn).astype(np.float64)
    else:
        nib = np.empty((g, p, n, 4), np.uint8)
        nib[..., 0::2] = words & 0xF
        nib[..., 1::2] = words >> 4
        vals = E2M1[nib]
    vals = vals * np.repeat(np.exp2(scales.astype(np.float64) - 127.0), 8, axis=1)[..., None]
    return vals.transpose(0, 1, 3, 2).reshape(g * 512, n)
def pack4(w):
    words, scales = pack_weight(w, "e2m1")
    return words.reshape(words.shape[0], 128, -1), scales


def unpack4(words, scales):
    return unpack_weight(words.reshape(words.shape[0], 128, -1, 2), scales, "e2m1")


P, F, J, C, V = 2048, 1024, 1024, 512, 1024


def setup_inputs():
    s, u, t = mx_kscale(F), mx_kscale(C), mx_kscale(J)
    normals = np.random.standard_normal((F, P)) * s[:, None]
    halves = np.random.standard_normal((F, J)) / np.sqrt(F) / s[:, None]
    normal_words, normal_scales = pack4(normals)
    half_words, half_scales = pack4(halves)
    return {"normal_words": normal_words,
            "normal_scales": normal_scales,
            "half_words": half_words,
            "half_scales": half_scales,
            "falloff": bf((0.5 + np.random.random_sample(J)) / J ** 0.25 * t),
            "emission": bf(np.random.standard_normal((J, C)) / J ** 0.25 * u / t[:, None]),
            "basis": bf(np.random.standard_normal((C, V)) / np.sqrt(C) / u[:, None])}


def reference(normal_words, normal_scales, half_words, half_scales, falloff, emission, basis):
    normals = unpack4(normal_words, normal_scales)
    halves = unpack4(half_words, half_scales)
    z = normals.T @ halves
    lobe = np.square(np.maximum(z, 0.0)) * f64(falloff)[None, :]
    radiance = mxq(f64(emission), 1, "e4m3") @ mxq(f64(basis), 0, "e4m3")
    return mxq(lobe, 1, "e4m3") @ mxq(radiance, 0, "e4m3")

@@ -1,0 +1,329 @@
+from contextlib import ExitStack
+
+import concourse.mybir as mybir
+from concourse.masks import make_identity
+
+POINTS, FEATS, LIGHTS, COEFS, BANDS = 2048, 1024, 1024, 512, 1024
+FLOPS = 2 * (POINTS * FEATS * LIGHTS + LIGHTS * COEFS * BANDS + POINTS * LIGHTS * BANDS)
+
+F32 = mybir.dt.float32
+BF16 = mybir.dt.bfloat16
+I32 = mybir.dt.int32
+U32 = mybir.dt.uint32
+U8 = mybir.dt.uint8
+FP8X4 = mybir.dt.float8_e4m3fn_x4
+FP4X4 = mybir.dt.float4_e2m1fn_x4
+ALU = mybir.AluOpType
+ACT = mybir.ActivationFunctionType
+
+P = 128
+N = 512
+CHUNKS = POINTS // N
+HALF = N // 2
+SQRT_FLOOR = 2.0 ** -110
+
+
+def tile_blinn_phong_radiance_s12_kernel(
+    tc, normal_words, normal_scales, half_words, half_scales, falloff, emission, basis, out
+):
+    nc = tc.nc
+    with ExitStack() as ctx:
+        keep = ctx.enter_context(tc.tile_pool(name="keep", bufs=1))
+        ring = ctx.enter_context(tc.tile_pool(name="ring", bufs=4))
+        psum = ctx.enter_context(tc.psum_pool(name="psum", bufs=8))
+        ctx.enter_context(tc.manual_schedule())
+
+        def kept(name, shape, dtype):
+            return keep.tile(shape, dtype, name=name, align_bytes=64)
+
+        def bank(shape, dtype):
+            return psum.tile(shape, dtype, name="bank", tag="bank")
+
+        ident_b = kept("ident_b", [P, P], BF16)
+        ident_f = kept("ident_f", [P, P], F32)
+        make_identity(nc, ident_b[:])
+        make_identity(nc, ident_f[:])
+
+        f_rows = kept("f_rows", [P, 2 * P], BF16)
+        hs_raw = kept("hs_raw", [P, 2, LIGHTS], U8)
+        ns_first = kept("ns_first", [P, 2, N], U8)
+        ns_rest = kept("ns_rest", [P, 2, POINTS - N], U8)
+        nc.vector.memset(f_rows[:], 0.0)
+        for plane in (hs_raw, ns_first, ns_rest):
+            nc.vector.memset(plane[:].bitcast(I32), 0)
+
+        def load_words(name, src, col0):
+            t = kept(name, [P, 2, 2 * N], U8)
+            view = src.rearrange("g p n -> p g n")[:, :, 2 * col0 : 2 * (col0 + N)]
+            nc.sync.dma_start(out=t[:].bitcast(I32), in_=view.bitcast(I32))
+            return t
+
+        def load_scales(plane, src, col0, width):
+            for quad in range(4):
+                view = src[:, 4 * quad : 4 * quad + 4, col0 : col0 + width].rearrange("g r n -> r g n")
+                nc.sync.dma_start(out=plane[32 * quad : 32 * quad + 4].bitcast(I32), in_=view.bitcast(I32))
+
+        hw_raw = [None, None]
+        nw = [None] * CHUNKS
+        hw_raw[0] = load_words("hw_raw0", half_words, 0)
+        nc.sync.dma_start(
+            out=f_rows[0:4, :].rearrange("t (a r) -> t a r", r=8),
+            in_=falloff.rearrange("(a t r) -> t a r", t=4, r=8),
+        )
+        load_scales(hs_raw, half_scales, 0, LIGHTS)
+        nw[0] = load_words("nw0", normal_words, 0)
+        load_scales(ns_first, normal_scales, 0, N)
+        hw_raw[1] = load_words("hw_raw1", half_words, N)
+        f_nat = kept("f_nat", [P, 2, 4], BF16)
+        nc.sync.dma_start(out=f_nat[:], in_=falloff.rearrange("(G p i) -> p G i", G=2, i=4))
+        b_raw, e_raw = [], []
+        for vh in range(2):
+            t = kept("b_raw%d" % vh, [P, 4, N], BF16)
+            nc.sync.dma_start(out=t[:], in_=basis.rearrange("(p t) v -> p t v", t=4)[:, :, vh * N : (vh + 1) * N])
+            b_raw.append(t)
+        for G in range(2):
+            t = kept("e_raw%d" % G, [P, 4, COEFS], BF16)
+            nc.sync.dma_start(out=t[:], in_=emission[G * N : (G + 1) * N, :].rearrange("(p i) c -> p i c", i=4))
+            e_raw.append(t)
+        nw[1] = load_words("nw1", normal_words, N)
+        load_scales(ns_rest, normal_scales, N, POINTS - N)
+        for c in range(2, CHUNKS):
+            nw[c] = load_words("nw%d" % c, normal_words, c * N)
+
+        f_ps = bank([P, 2, P], BF16)
+        for G in range(2):
+            nc.tensor.transpose(f_ps[:, G, :], f_rows[:, G * P : (G + 1) * P], ident_b[:])
+
+        hw = [kept("hw%d" % G, [P, 2, 2 * N], U8) for G in range(2)]
+        hs = kept("hs", [P, 2, LIGHTS], U8)
+
+        def sort_half_words(G):
+            nc.vector.tensor_copy(
+                out=hw[G][:].bitcast(I32).rearrange("p g (t q k) -> p g t q k", t=4, k=4),
+                in_=hw_raw[G][:].bitcast(I32).rearrange("p g (q t k) -> p g t q k", t=4, k=4),
+            )
+
+        sort_half_words(0)
+        nc.vector.tensor_copy(
+            out=hs[:].bitcast(I32).rearrange("p g (G t q k) -> p (g G) t q k", G=2, t=4, k=2),
+            in_=hs_raw[:].bitcast(I32).rearrange("p g (G q t k) -> p (g G) t q k", G=2, t=4, k=2),
+        )
+
+        f_val = f_ps[:, :, 0:4]
+        f_neg = kept("f_neg", [P, 2, 4], F32)
+        f_abs = kept("f_abs", [P, 2, 4], F32)
+        f_low = kept("f_low", [P, 2, 4], F32)
+        guess = kept("guess", [P, 2, 4], F32)
+        half_nz = kept("half_nz", [P, 2, 4], F32)
+        inv = kept("inv", [P, 2, 4], F32)
+        term_a = kept("term_a", [P, 2, 4], F32)
+        term_b = kept("term_b", [P, 2, 4], F32)
+        root = kept("root", [P, 2, 4], F32)
+        nc.vector.tensor_scalar(f_neg[:], f_val, -1.0, None, ALU.mult)
+        nc.vector.scalar_tensor_tensor(f_low[:], f_val, SQRT_FLOOR, f_neg[:], ALU.max, ALU.max)
+        nc.scalar.activation(guess[:], f_low[:], ACT.Sqrt)
+        nc.vector.tensor_tensor(f_abs[:], f_val, f_neg[:], ALU.max)
+        nc.vector.tensor_scalar(half_nz[:], f_abs[:], 0.0, 0.5, ALU.is_gt, ALU.mult)
+        nc.vector.reciprocal(inv[:], guess[:])
+        nc.vector.tensor_tensor(term_a[:], guess[:], half_nz[:], ALU.mult)
+        nc.vector.scalar_tensor_tensor(term_b[:], f_abs[:], 0.5, inv[:], ALU.mult, ALU.mult)
+        nc.vector.tensor_tensor(root[:], term_a[:], term_b[:], ALU.add)
+
+        sign2 = kept("sign2", [P, 2, 4], F32)
+        sign = kept("sign", [P, 2, 4], F32)
+
+        def falloff_sign():
+            nc.vector.tensor_scalar(sign2[:], f_nat[:], 0.0, 2.0, ALU.is_ge, ALU.mult)
+            nc.vector.tensor_scalar(sign[:], sign2[:], -1.0, None, ALU.add)
+
+        def quantize(name, src):
+            width = src.shape[1] // 4
+            codes = kept(name + "_codes", [P, width], U32)
+            scales = kept(name + "_scales", [P, width], U8)
+            nc.vector.quantize_mx(out=codes[:].bitcast(FP8X4), scales=scales[:], in_=src)
+            return codes, scales
+
+        def copy_out(engine, dst, src):
+            if engine == "V":
+                nc.vector.tensor_copy(out=dst, in_=src)
+            else:
+                nc.scalar.copy(out=dst, in_=src)
+
+        b_bf = [kept("b_bf%d" % vh, [P, N, 4], BF16) for vh in range(2)]
+        b_mx = {}
+
+        def basis_interleave(vh):
+            nc.vector.tensor_copy(
+                out=b_bf[vh][:].rearrange("p (c i) t -> p c t i", i=4),
+                in_=b_raw[vh][:].rearrange("p t (c i) -> p c t i", i=4),
+            )
+
+        def basis_quantize(vh):
+            b_mx[vh] = quantize("b%d" % vh, b_bf[vh][:].rearrange("p v t -> p (v t)"))
+
+        e_sgn = [kept("e_sgn%d" % G, [P, 4 * COEFS], BF16) for G in range(2)]
+        e_bf = [kept("e_bf%d" % G, [P, 4 * N], BF16) for G in range(2)]
+        e_mx = {}
+
+        def emission_sign(G):
+            for i in range(4):
+                nc.vector.tensor_scalar(
+                    e_sgn[G][:, i * COEFS : (i + 1) * COEFS], e_raw[G][:, i, :], sign[:, G, i : i + 1], None, ALU.mult
+                )
+
+        def emission_turn(G, b):
+            ps = bank([P, 4, P], F32)
+            words = e_sgn[G][:].bitcast(F32)
+            for x in range(4):
+                i, u = 2 * b + x // 2, x % 2
+                nc.tensor.transpose(ps[:, x, :], words[:, 256 * i + u : 256 * (i + 1) : 2], ident_f[:])
+            dst = e_bf[G][:].bitcast(F32).rearrange("p (t q h b x) -> p b t q h x", t=4, h=2, b=2, x=4)
+            nc.vector.tensor_copy(out=dst[:, b], in_=ps[:].rearrange("p x (q t h) -> p t q h x", t=4, h=2))
+
+        def emission_quantize(G):
+            e_mx[G] = quantize("e%d" % G, e_bf[G][:])
+
+        r_bf = {(G, vh): kept("r_bf%d%d" % (G, vh), [P, N, 4], BF16) for G in range(2) for vh in range(2)}
+        r_mx = {}
+
+        def radiance(G, vb, engine):
+            vh, cols = vb // 4, slice((vb % 4) * P, (vb % 4 + 1) * P)
+            ps = bank([P, 4, P], F32)
+            for t in range(4):
+                ts = slice(t * P, (t + 1) * P)
+                nc.tensor.matmul_mx(
+                    out=ps[:, t, :],
+                    lhsT=e_mx[G][0][:, ts].bitcast(FP8X4),
+                    lhsT_scale=e_mx[G][1][:, ts],
+                    rhs=b_mx[vh][0][:, cols].bitcast(FP8X4),
+                    rhs_scale=b_mx[vh][1][:, cols],
+                    start=True,
+                    stop=True,
+                )
+            copy_out(engine, r_bf[G, vh][:, cols, :], ps[:].rearrange("p t n -> p n t"))
+
+        def radiance_quantize(G, vh):
+            r_mx[G, vh] = quantize("r%d%d" % (G, vh), r_bf[G, vh][:].rearrange("p v t -> p (v t)"))
+
+        relu_t, lobe_bf, lobe_mx = {}, {}, {}
+
+        def cosines(c, G, t, engine):
+            if t == 0:
+                relu_t[c, G] = ring.tile([P, 4, N], F32, name="relu_t", tag="relu_t")
+            ps = bank([P, N], F32)
+            for g in range(2):
+                n_scale = ns_first[:, g, :] if c == 0 else ns_rest[:, g, (c - 1) * N : c * N]
+                nc.tensor.matmul_mx(
+                    out=ps[:],
+                    lhsT=hw[G][:, g, 2 * t * P : 2 * (t + 1) * P].bitcast(FP4X4),
+                    lhsT_scale=hs[:, g, G * N + t * P : G * N + (t + 1) * P],
+                    rhs=nw[c][:, g, :].bitcast(FP4X4),
+                    rhs_scale=n_scale,
+                    start=(g == 0),
+                    stop=(g == 1),
+                )
+            if engine == "V":
+                nc.vector.tensor_scalar(relu_t[c, G][:, t, :], ps[:], root[:, G, t : t + 1], 0.0, ALU.mult, ALU.max)
+            else:
+                nc.scalar.activation(relu_t[c, G][:, t, :], ps[:], ACT.Relu, scale=root[:, G, t : t + 1])
+
+        def square(c, G):
+            for h in range(2):
+                t = ring.tile([P, HALF, 4], BF16, name="lobe_bf", tag="lobe_bf", align_bytes=64)
+                lobe_bf[c, G, h] = t
+                nc.scalar.activation(
+                    t[:].rearrange("p (c i) t -> p c t i", i=4),
+                    relu_t[c, G][:, :, h * HALF : (h + 1) * HALF].rearrange("p t (c i) -> p c t i", i=4),
+                    ACT.Square,
+                )
+
+        def lobe_quantize(c, G):
+            for h in range(2):
+                lobe_mx[c, G, h] = quantize("l%d%d%d" % (c, G, h), lobe_bf[c, G, h][:].rearrange("p n t -> p (n t)"))
+
+        def shade(c, pt, vh, engine):
+            ps = bank([P, N], F32)
+            cols = slice((pt % 2) * P, (pt % 2 + 1) * P)
+            for G in range(2):
+                codes, scales = lobe_mx[c, G, pt // 2]
+                nc.tensor.matmul_mx(
+                    out=ps[:],
+                    lhsT=codes[:, cols].bitcast(FP8X4),
+                    lhsT_scale=scales[:, cols],
+                    rhs=r_mx[G, vh][0][:].bitcast(FP8X4),
+                    rhs_scale=r_mx[G, vh][1][:],
+                    start=(G == 0),
+                    stop=(G == 1),
+                )
+            res = ring.tile([P, N], F32, name="res", tag="res", bufs=10)
+            copy_out(engine, res[:], ps[:])
+            row0 = c * N + pt * P
+            nc.sync.dma_start(out=out[row0 : row0 + P, vh * N : (vh + 1) * N], in_=res[:])
+
+        cosines(0, 0, 0, "S")
+        cosines(0, 0, 1, "S")
+        sort_half_words(1)
+        falloff_sign()
+        cosines(0, 0, 2, "S")
+        cosines(0, 0, 3, "S")
+        basis_interleave(0)
+        basis_interleave(1)
+        for t in range(4):
+            cosines(0, 1, t, "S")
+        emission_sign(0)
+        basis_quantize(0)
+        emission_sign(1)
+        basis_quantize(1)
+        square(0, 0)
+        emission_turn(0, 0)
+        emission_turn(0, 1)
+        emission_turn(1, 0)
+        emission_quantize(0)
+        emission_turn(1, 1)
+        lobe_quantize(0, 0)
+        emission_quantize(1)
+        square(0, 1)
+        for t in range(4):
+            cosines(1, 0, t, "V")
+        for vb in range(4):
+            radiance(0, vb, "SV"[vb % 2])
+        radiance(1, 0, "S")
+        lobe_quantize(0, 1)
+        radiance(1, 1, "S")
+        radiance_quantize(0, 0)
+        radiance(1, 2, "S")
+        radiance(1, 3, "V")
+        cosines(1, 1, 0, "S")
+        cosines(1, 1, 1, "V")
+        radiance_quantize(1, 0)
+        cosines(1, 1, 2, "S")
+        cosines(1, 1, 3, "V")
+        for vb in range(4, 8):
+            radiance(0, vb, "VS"[vb % 2])
+        shade(0, 0, 0, "V")
+        radiance(1, 4, "S")
+        radiance_quantize(0, 1)
+        radiance(1, 5, "V")
+        shade(0, 1, 0, "V")
+        radiance(1, 6, "S")
+        radiance(1, 7, "V")
+        square(1, 0)
+        shade(0, 2, 0, "V")
+        radiance_quantize(1, 1)
+        shade(0, 3, 0, "V")
+        cosines(2, 0, 0, "V")
+        cosines(2, 0, 1, "V")
+        lobe_quantize(1, 0)
+        square(1, 1)
+        shades = [(0, pt, 1) for pt in range(4)] + [(c, pt, vh) for c in (1, 2, 3) for pt in range(4) for vh in range(2)]
+        zs = [(2, 0, 2), (2, 0, 3)] + [(2, 1, t) for t in range(4)] + [(3, G, t) for G in range(2) for t in range(4)]
+        squares = {2: (2, 0), 6: (2, 1), 10: (3, 0), 13: (3, 1)}
+        quants = {2: (1, 1), 4: (2, 0), 8: (2, 1), 12: (3, 0), 17: (3, 1)}
+        for i, s in enumerate(shades):
+            shade(s[0], s[1], s[2], "V" if 14 <= i <= 17 else "SV"[i % 2])
+            if i < len(zs):
+                cosines(zs[i][0], zs[i][1], zs[i][2], "V")
+            if i in quants:
+                lobe_quantize(quants[i][0], quants[i][1])
+            if i in squares:
+                square(squares[i][0], squares[i][1])

@@ -20,6 +20,7 @@ P = 128
 N = 512
 CHUNKS = POINTS // N
 HALF = N // 2
+HALVES = (slice(0, N), slice(N, 2 * N))
 SQRT_FLOOR = 2.0 ** -110
 
 
@@ -46,11 +47,9 @@ def tile_blinn_phong_radiance_s12_kernel(
 
         f_rows = kept("f_rows", [P, 2 * P], BF16)
         hs_raw = kept("hs_raw", [P, 2, LIGHTS], U8)
-        ns_first = kept("ns_first", [P, 2, N], U8)
-        ns_rest = kept("ns_rest", [P, 2, POINTS - N], U8)
-        nc.vector.memset(f_rows[:], 0.0)
-        for plane in (hs_raw, ns_first, ns_rest):
-            nc.vector.memset(plane[:].bitcast(I32), 0)
+        ns = [kept("ns%d" % i, [P, 2, 2 * N], U8) for i in range(2)]
+        for filled in (f_rows, hs_raw, ns[0], ns[1]):
+            nc.vector.memset(filled[:].bitcast(I32), 0)
 
         def load_words(name, src, col0):
             t = kept(name, [P, 2, 2 * N], U8)
@@ -72,23 +71,28 @@ def tile_blinn_phong_radiance_s12_kernel(
         )
         load_scales(hs_raw, half_scales, 0, LIGHTS)
         nw[0] = load_words("nw0", normal_words, 0)
-        load_scales(ns_first, normal_scales, 0, N)
+        load_scales(ns[0], normal_scales, 0, 2 * N)
         hw_raw[1] = load_words("hw_raw1", half_words, N)
-        f_nat = kept("f_nat", [P, 2, 4], BF16)
-        nc.sync.dma_start(out=f_nat[:], in_=falloff.rearrange("(G p i) -> p G i", G=2, i=4))
-        b_raw, e_raw = [], []
-        for vh in range(2):
+
+        def load_basis(vh):
             t = kept("b_raw%d" % vh, [P, 4, N], BF16)
             nc.sync.dma_start(out=t[:], in_=basis.rearrange("(p t) v -> p t v", t=4)[:, :, vh * N : (vh + 1) * N])
-            b_raw.append(t)
-        for G in range(2):
-            t = kept("e_raw%d" % G, [P, 4, COEFS], BF16)
-            nc.sync.dma_start(out=t[:], in_=emission[G * N : (G + 1) * N, :].rearrange("(p i) c -> p i c", i=4))
-            e_raw.append(t)
+            return t
+
+        def load_emission(G):
+            t = kept("e_raw%d" % G, [P, 4 * COEFS], BF16)
+            nc.sync.dma_start(out=t[:], in_=emission[G * N : (G + 1) * N, :].rearrange("(p i) c -> p (i c)", i=4))
+            return t
+
+        b_raw, e_raw = [None, None], [None, None]
+        b_raw[0] = load_basis(0)
+        e_raw[0] = load_emission(0)
         nw[1] = load_words("nw1", normal_words, N)
-        load_scales(ns_rest, normal_scales, N, POINTS - N)
-        for c in range(2, CHUNKS):
-            nw[c] = load_words("nw%d" % c, normal_words, c * N)
+        e_raw[1] = load_emission(1)
+        b_raw[1] = load_basis(1)
+        nw[2] = load_words("nw2", normal_words, 2 * N)
+        load_scales(ns[1], normal_scales, 2 * N, 2 * N)
+        nw[3] = load_words("nw3", normal_words, 3 * N)
 
         f_ps = bank([P, 2, P], BF16)
         for G in range(2):
@@ -133,7 +137,7 @@ def tile_blinn_phong_radiance_s12_kernel(
         sign = kept("sign", [P, 2, 4], F32)
 
         def falloff_sign():
-            nc.vector.tensor_scalar(sign2[:], f_nat[:], 0.0, 2.0, ALU.is_ge, ALU.mult)
+            nc.vector.tensor_scalar(sign2[:], f_neg[:], 0.0, 2.0, ALU.is_le, ALU.mult)
             nc.vector.tensor_scalar(sign[:], sign2[:], -1.0, None, ALU.add)
 
         def quantize(name, src):
@@ -161,24 +165,17 @@ def tile_blinn_phong_radiance_s12_kernel(
         def basis_quantize(vh):
             b_mx[vh] = quantize("b%d" % vh, b_bf[vh][:].rearrange("p v t -> p (v t)"))
 
-        e_sgn = [kept("e_sgn%d" % G, [P, 4 * COEFS], BF16) for G in range(2)]
         e_bf = [kept("e_bf%d" % G, [P, 4 * N], BF16) for G in range(2)]
         e_mx = {}
 
-        def emission_sign(G):
-            for i in range(4):
-                nc.vector.tensor_scalar(
-                    e_sgn[G][:, i * COEFS : (i + 1) * COEFS], e_raw[G][:, i, :], sign[:, G, i : i + 1], None, ALU.mult
-                )
-
         def emission_turn(G, b):
             ps = bank([P, 4, P], F32)
-            words = e_sgn[G][:].bitcast(F32)
+            words = e_raw[G][:].bitcast(F32)
             for x in range(4):
                 i, u = 2 * b + x // 2, x % 2
                 nc.tensor.transpose(ps[:, x, :], words[:, 256 * i + u : 256 * (i + 1) : 2], ident_f[:])
             dst = e_bf[G][:].bitcast(F32).rearrange("p (t q h b x) -> p b t q h x", t=4, h=2, b=2, x=4)
-            nc.vector.tensor_copy(out=dst[:, b], in_=ps[:].rearrange("p x (q t h) -> p t q h x", t=4, h=2))
+            nc.scalar.copy(out=dst[:, b], in_=ps[:].rearrange("p x (q t h) -> p t q h x", t=4, h=2))
 
         def emission_quantize(G):
             e_mx[G] = quantize("e%d" % G, e_bf[G][:])
@@ -186,7 +183,7 @@ def tile_blinn_phong_radiance_s12_kernel(
         r_bf = {(G, vh): kept("r_bf%d%d" % (G, vh), [P, N, 4], BF16) for G in range(2) for vh in range(2)}
         r_mx = {}
 
-        def radiance(G, vb, engine):
+        def radiance(G, vb):
             vh, cols = vb // 4, slice((vb % 4) * P, (vb % 4 + 1) * P)
             ps = bank([P, 4, P], F32)
             for t in range(4):
@@ -200,7 +197,12 @@ def tile_blinn_phong_radiance_s12_kernel(
                     start=True,
                     stop=True,
                 )
-            copy_out(engine, r_bf[G, vh][:, cols, :], ps[:].rearrange("p t n -> p n t"))
+            nc.vector.tensor_tensor(
+                r_bf[G, vh][:, cols, :],
+                ps[:].rearrange("p t n -> p n t"),
+                sign[:, G, :].unsqueeze(1).to_broadcast([P, P, 4]),
+                ALU.mult,
+            )
 
         def radiance_quantize(G, vh):
             r_mx[G, vh] = quantize("r%d%d" % (G, vh), r_bf[G, vh][:].rearrange("p v t -> p (v t)"))
@@ -209,10 +211,10 @@ def tile_blinn_phong_radiance_s12_kernel(
 
         def cosines(c, G, t, engine):
             if t == 0:
-                relu_t[c, G] = ring.tile([P, 4, N], F32, name="relu_t", tag="relu_t")
+                relu_t[c, G] = ring.tile([P, 4, N], F32, name="relu_t", tag="relu_t", bufs=5)
             ps = bank([P, N], F32)
             for g in range(2):
-                n_scale = ns_first[:, g, :] if c == 0 else ns_rest[:, g, (c - 1) * N : c * N]
+                n_scale = ns[c // 2][:, g, (c % 2) * N : (c % 2 + 1) * N]
                 nc.tensor.matmul_mx(
                     out=ps[:],
                     lhsT=hw[G][:, g, 2 * t * P : 2 * (t + 1) * P].bitcast(FP4X4),
@@ -227,103 +229,153 @@ def tile_blinn_phong_radiance_s12_kernel(
             else:
                 nc.scalar.activation(relu_t[c, G][:, t, :], ps[:], ACT.Relu, scale=root[:, G, t : t + 1])
 
-        def square(c, G):
-            for h in range(2):
-                t = ring.tile([P, HALF, 4], BF16, name="lobe_bf", tag="lobe_bf", align_bytes=64)
-                lobe_bf[c, G, h] = t
-                nc.scalar.activation(
-                    t[:].rearrange("p (c i) t -> p c t i", i=4),
-                    relu_t[c, G][:, :, h * HALF : (h + 1) * HALF].rearrange("p t (c i) -> p c t i", i=4),
-                    ACT.Square,
-                )
+        def square(c, G, h):
+            if h == 0:
+                lobe_bf[c, G] = ring.tile([P, N, 4], BF16, name="lobe_bf", tag="lobe_bf", align_bytes=64)
+                lobe_mx[c, G] = (kept("l%d%d_codes" % (c, G), [P, N], U32), kept("l%d%d_scales" % (c, G), [P, N], U8))
+            cols = slice(h * HALF, (h + 1) * HALF)
+            nc.scalar.activation(
+                lobe_bf[c, G][:, cols, :].rearrange("p (c i) t -> p c t i", i=4),
+                relu_t[c, G][:, :, cols].rearrange("p t (c i) -> p c t i", i=4),
+                ACT.Square,
+            )
 
-        def lobe_quantize(c, G):
-            for h in range(2):
-                lobe_mx[c, G, h] = quantize("l%d%d%d" % (c, G, h), lobe_bf[c, G, h][:].rearrange("p n t -> p (n t)"))
+        def lobe_quantize(c, G, cols=slice(0, N)):
+            codes, scales = lobe_mx[c, G]
+            nc.vector.quantize_mx(
+                out=codes[:, cols].bitcast(FP8X4),
+                scales=scales[:, cols],
+                in_=lobe_bf[c, G][:, cols, :].rearrange("p n t -> p (n t)"),
+            )
 
-        def shade(c, pt, vh, engine):
-            ps = bank([P, N], F32)
-            cols = slice((pt % 2) * P, (pt % 2 + 1) * P)
+        def shade_columns(c, pt, bands, dst, engine):
+            ps = bank([P, bands.stop - bands.start], F32)
+            vh = bands.start // N
+            moving = slice(bands.start - vh * N, bands.stop - vh * N)
+            cols = slice(pt * P, (pt + 1) * P)
             for G in range(2):
-                codes, scales = lobe_mx[c, G, pt // 2]
+                codes, scales = lobe_mx[c, G]
                 nc.tensor.matmul_mx(
                     out=ps[:],
                     lhsT=codes[:, cols].bitcast(FP8X4),
                     lhsT_scale=scales[:, cols],
-                    rhs=r_mx[G, vh][0][:].bitcast(FP8X4),
-                    rhs_scale=r_mx[G, vh][1][:],
+                    rhs=r_mx[G, vh][0][:, moving].bitcast(FP8X4),
+                    rhs_scale=r_mx[G, vh][1][:, moving],
                     start=(G == 0),
                     stop=(G == 1),
                 )
-            res = ring.tile([P, N], F32, name="res", tag="res", bufs=10)
-            copy_out(engine, res[:], ps[:])
-            row0 = c * N + pt * P
-            nc.sync.dma_start(out=out[row0 : row0 + P, vh * N : (vh + 1) * N], in_=res[:])
+            copy_out(engine, dst, ps[:])
 
-        cosines(0, 0, 0, "S")
-        cosines(0, 0, 1, "S")
+        def store(c, pt, bands, res):
+            nc.sync.dma_start(out=out[c * N + pt * P : c * N + (pt + 1) * P, bands], in_=res[:, bands])
+
+        def staging():
+            return ring.tile([P, BANDS], F32, name="res", tag="res", bufs=6)
+
+        def shade(c, pt, bands, engine):
+            res = staging()
+            shade_columns(c, pt, bands, res[:, bands], engine)
+            store(c, pt, bands, res)
+
+        def shade_rows(c, pt, engines):
+            res = staging()
+            for vh in range(2):
+                shade_columns(c, pt, HALVES[vh], res[:, HALVES[vh]], engines[vh])
+            store(c, pt, slice(0, BANDS), res)
+
         sort_half_words(1)
         falloff_sign()
+        cosines(0, 0, 0, "S")
+        cosines(0, 0, 1, "V")
         cosines(0, 0, 2, "S")
-        cosines(0, 0, 3, "S")
         basis_interleave(0)
-        basis_interleave(1)
-        for t in range(4):
-            cosines(0, 1, t, "S")
-        emission_sign(0)
+        cosines(0, 0, 3, "S")
+        cosines(0, 1, 0, "V")
+        square(0, 0, 0)
+        cosines(0, 1, 1, "V")
         basis_quantize(0)
-        emission_sign(1)
-        basis_quantize(1)
-        square(0, 0)
+        square(0, 0, 1)
+        cosines(0, 1, 2, "V")
+        cosines(0, 1, 3, "V")
+
         emission_turn(0, 0)
         emission_turn(0, 1)
+        lobe_quantize(0, 0)
+        cosines(1, 0, 0, "V")
+        basis_interleave(1)
+        cosines(1, 0, 1, "S")
         emission_turn(1, 0)
         emission_quantize(0)
         emission_turn(1, 1)
-        lobe_quantize(0, 0)
+        cosines(1, 0, 2, "V")
+        square(0, 1, 0)
+        basis_quantize(1)
+        cosines(1, 0, 3, "V")
         emission_quantize(1)
-        square(0, 1)
-        for t in range(4):
-            cosines(1, 0, t, "V")
-        for vb in range(4):
-            radiance(0, vb, "SV"[vb % 2])
-        radiance(1, 0, "S")
-        lobe_quantize(0, 1)
-        radiance(1, 1, "S")
-        radiance_quantize(0, 0)
-        radiance(1, 2, "S")
-        radiance(1, 3, "V")
-        cosines(1, 1, 0, "S")
-        cosines(1, 1, 1, "V")
-        radiance_quantize(1, 0)
-        cosines(1, 1, 2, "S")
-        cosines(1, 1, 3, "V")
-        for vb in range(4, 8):
-            radiance(0, vb, "VS"[vb % 2])
-        shade(0, 0, 0, "V")
-        radiance(1, 4, "S")
-        radiance_quantize(0, 1)
-        radiance(1, 5, "V")
-        shade(0, 1, 0, "V")
-        radiance(1, 6, "S")
-        radiance(1, 7, "V")
-        square(1, 0)
-        shade(0, 2, 0, "V")
+        square(0, 1, 1)
+
+        groups = [(G, vh) for vh in range(2) for G in range(2)]
+        beside = [(1, 1), (2, 0), (2, 1)]
+        for k, (G, vh) in enumerate(groups):
+            for i in range(4):
+                radiance(G, 4 * vh + i)
+                if k < len(beside):
+                    cosines(beside[k][0], beside[k][1], i, "S")
+                else:
+                    shade(0, i, HALVES[0], "S")
+                if i == 0 and k > 0:
+                    radiance_quantize(groups[k - 1][0], groups[k - 1][1])
+                if i == 2 and k == 0:
+                    lobe_quantize(0, 1)
+                if i == 2 and k == 2:
+                    lobe_quantize(1, 0)
+            square(1, k // 2, k % 2)
+
+        cosines(3, 0, 0, "V")
         radiance_quantize(1, 1)
-        shade(0, 3, 0, "V")
-        cosines(2, 0, 0, "V")
-        cosines(2, 0, 1, "V")
-        lobe_quantize(1, 0)
-        square(1, 1)
-        shades = [(0, pt, 1) for pt in range(4)] + [(c, pt, vh) for c in (1, 2, 3) for pt in range(4) for vh in range(2)]
-        zs = [(2, 0, 2), (2, 0, 3)] + [(2, 1, t) for t in range(4)] + [(3, G, t) for G in range(2) for t in range(4)]
-        squares = {2: (2, 0), 6: (2, 1), 10: (3, 0), 13: (3, 1)}
-        quants = {2: (1, 1), 4: (2, 0), 8: (2, 1), 12: (3, 0), 17: (3, 1)}
-        for i, s in enumerate(shades):
-            shade(s[0], s[1], s[2], "V" if 14 <= i <= 17 else "SV"[i % 2])
-            if i < len(zs):
-                cosines(zs[i][0], zs[i][1], zs[i][2], "V")
-            if i in quants:
-                lobe_quantize(quants[i][0], quants[i][1])
-            if i in squares:
-                square(squares[i][0], squares[i][1])
+        cosines(3, 0, 1, "V")
+        square(2, 0, 0)
+        cosines(3, 0, 2, "V")
+        lobe_quantize(1, 1)
+        cosines(3, 0, 3, "V")
+        square(2, 0, 1)
+        for pt in range(4):
+            shade(0, pt, HALVES[1], "VS"[pt % 2])
+            if pt == 2:
+                lobe_quantize(2, 0)
+        square(2, 1, 0)
+
+        for pt in range(4):
+            shade_rows(1, pt, "VV" if pt == 0 else "VS")
+            cosines(3, 1, pt, "V")
+            if pt == 0:
+                square(2, 1, 1)
+            elif pt == 1:
+                lobe_quantize(2, 1)
+                square(3, 0, 0)
+            elif pt == 2:
+                square(3, 0, 1)
+        lobe_quantize(3, 0)
+
+        res = staging()
+        shade_columns(2, 0, HALVES[0], res[:, HALVES[0]], "S")
+        square(3, 1, 0)
+        shade_columns(2, 0, HALVES[1], res[:, HALVES[1]], "V")
+        store(2, 0, slice(0, BANDS), res)
+        res = staging()
+        shade_columns(2, 1, HALVES[0], res[:, HALVES[0]], "V")
+        square(3, 1, 1)
+        lobe_quantize(3, 1, slice(0, HALF))
+        shade_columns(2, 1, HALVES[1], res[:, HALVES[1]], "V")
+        store(2, 1, slice(0, BANDS), res)
+        res = staging()
+        shade_columns(2, 2, HALVES[0], res[:, HALVES[0]], "V")
+        lobe_quantize(3, 1, slice(HALF, N))
+        shade_columns(2, 2, HALVES[1], res[:, HALVES[1]], "S")
+        store(2, 2, slice(0, BANDS), res)
+        shade_rows(2, 3, "VS")
+        for pt in range(3):
+            shade_rows(3, pt, "VS")
+        shade(3, 3, HALVES[0], "V")
+        shade(3, 3, slice(N, N + HALF), "S")
+        shade(3, 3, slice(N + HALF, BANDS), "V")

@@ -42,14 +42,35 @@ def tile_blinn_phong_radiance_s12_kernel(
 
         ident_b = kept("ident_b", [P, P], BF16)
         ident_f = kept("ident_f", [P, P], F32)
-        make_identity(nc, ident_b[:])
-        make_identity(nc, ident_f[:])
 
         f_rows = kept("f_rows", [P, 2 * P], BF16)
         hs_raw = kept("hs_raw", [P, 2, LIGHTS], U8)
-        ns = [kept("ns%d" % i, [P, 2, 2 * N], U8) for i in range(2)]
-        for filled in (f_rows, hs_raw, ns[0], ns[1]):
-            nc.vector.memset(filled[:].bitcast(I32), 0)
+        ns_first = kept("ns_first", [P, 2, N], U8)
+        ns_rest = kept("ns_rest", [P, 2, POINTS - N], U8)
+        warm_bf = kept("warm_bf", [P, N], BF16)
+        nc.gpsimd.memset(f_rows[:].bitcast(I32), 0)
+        nc.vector.memset(warm_bf[:], 1.0)
+        nc.vector.memset(hs_raw[:].bitcast(I32), 0)
+        make_identity(nc, ident_b[:])
+        make_identity(nc, ident_f[:])
+        warm_codes = kept("warm_codes", [P, P], U32)
+        warm_scales = kept("warm_scales", [P, P], U8)
+        nc.vector.quantize_mx(out=warm_codes[:].bitcast(FP8X4), scales=warm_scales[:], in_=warm_bf[:])
+        nc.vector.memset(ns_first[:].bitcast(I32), 0)
+        nc.vector.memset(ns_rest[:].bitcast(I32), 0)
+        warm_ps = bank([P, 4, P], F32)
+
+        def warm_up(passes):
+            for i in range(passes):
+                nc.tensor.matmul_mx(
+                    out=warm_ps[:, i % 4, :],
+                    lhsT=warm_codes[:].bitcast(FP8X4),
+                    lhsT_scale=warm_scales[:],
+                    rhs=warm_codes[:].bitcast(FP8X4),
+                    rhs_scale=warm_scales[:],
+                    start=True,
+                    stop=True,
+                )
 
         def load_words(name, src, col0):
             t = kept(name, [P, 2, 2 * N], U8)
@@ -64,14 +85,14 @@ def tile_blinn_phong_radiance_s12_kernel(
 
         hw_raw = [None, None]
         nw = [None] * CHUNKS
-        hw_raw[0] = load_words("hw_raw0", half_words, 0)
         nc.sync.dma_start(
             out=f_rows[0:4, :].rearrange("t (a r) -> t a r", r=8),
             in_=falloff.rearrange("(a t r) -> t a r", t=4, r=8),
         )
         load_scales(hs_raw, half_scales, 0, LIGHTS)
+        hw_raw[0] = load_words("hw_raw0", half_words, 0)
         nw[0] = load_words("nw0", normal_words, 0)
-        load_scales(ns[0], normal_scales, 0, 2 * N)
+        load_scales(ns_first, normal_scales, 0, N)
         hw_raw[1] = load_words("hw_raw1", half_words, N)
 
         def load_basis(vh):
@@ -88,15 +109,17 @@ def tile_blinn_phong_radiance_s12_kernel(
         b_raw[0] = load_basis(0)
         e_raw[0] = load_emission(0)
         nw[1] = load_words("nw1", normal_words, N)
+        load_scales(ns_rest, normal_scales, N, POINTS - N)
         e_raw[1] = load_emission(1)
         b_raw[1] = load_basis(1)
         nw[2] = load_words("nw2", normal_words, 2 * N)
-        load_scales(ns[1], normal_scales, 2 * N, 2 * N)
         nw[3] = load_words("nw3", normal_words, 3 * N)
 
+        warm_up(10)
         f_ps = bank([P, 2, P], BF16)
         for G in range(2):
             nc.tensor.transpose(f_ps[:, G, :], f_rows[:, G * P : (G + 1) * P], ident_b[:])
+        warm_up(10)
 
         hw = [kept("hw%d" % G, [P, 2, 2 * N], U8) for G in range(2)]
         hs = kept("hs", [P, 2, LIGHTS], U8)
@@ -214,7 +237,7 @@ def tile_blinn_phong_radiance_s12_kernel(
                 relu_t[c, G] = ring.tile([P, 4, N], F32, name="relu_t", tag="relu_t", bufs=5)
             ps = bank([P, N], F32)
             for g in range(2):
-                n_scale = ns[c // 2][:, g, (c % 2) * N : (c % 2 + 1) * N]
+                n_scale = ns_first[:, g, :] if c == 0 else ns_rest[:, g, (c - 1) * N : c * N]
                 nc.tensor.matmul_mx(
                     out=ps[:],
                     lhsT=hw[G][:, g, 2 * t * P : 2 * (t + 1) * P].bitcast(FP4X4),
@@ -285,11 +308,9 @@ def tile_blinn_phong_radiance_s12_kernel(
 
         sort_half_words(1)
         falloff_sign()
-        cosines(0, 0, 0, "S")
-        cosines(0, 0, 1, "V")
-        cosines(0, 0, 2, "S")
         basis_interleave(0)
-        cosines(0, 0, 3, "S")
+        for t in range(4):
+            cosines(0, 0, t, "S")
         cosines(0, 1, 0, "V")
         square(0, 0, 0)
         cosines(0, 1, 1, "V")

@@ -49,14 +49,14 @@ def tile_blinn_phong_radiance_s12_kernel(
         ns_rest = kept("ns_rest", [P, 2, POINTS - N], U8)
         warm_bf = kept("warm_bf", [P, N], BF16)
         nc.gpsimd.memset(f_rows[:].bitcast(I32), 0)
+        nc.gpsimd.memset(hs_raw[:].bitcast(I32), 0)
+        nc.vector.memset(ns_first[:].bitcast(I32), 0)
         nc.vector.memset(warm_bf[:], 1.0)
-        nc.vector.memset(hs_raw[:].bitcast(I32), 0)
         make_identity(nc, ident_b[:])
         make_identity(nc, ident_f[:])
         warm_codes = kept("warm_codes", [P, P], U32)
         warm_scales = kept("warm_scales", [P, P], U8)
         nc.vector.quantize_mx(out=warm_codes[:].bitcast(FP8X4), scales=warm_scales[:], in_=warm_bf[:])
-        nc.vector.memset(ns_first[:].bitcast(I32), 0)
         nc.vector.memset(ns_rest[:].bitcast(I32), 0)
         warm_ps = bank([P, 4, P], F32)
 
@@ -108,9 +108,9 @@ def tile_blinn_phong_radiance_s12_kernel(
         b_raw, e_raw = [None, None], [None, None]
         b_raw[0] = load_basis(0)
         e_raw[0] = load_emission(0)
+        e_raw[1] = load_emission(1)
         nw[1] = load_words("nw1", normal_words, N)
         load_scales(ns_rest, normal_scales, N, POINTS - N)
-        e_raw[1] = load_emission(1)
         b_raw[1] = load_basis(1)
         nw[2] = load_words("nw2", normal_words, 2 * N)
         nw[3] = load_words("nw3", normal_words, 3 * N)
@@ -119,7 +119,7 @@ def tile_blinn_phong_radiance_s12_kernel(
         f_ps = bank([P, 2, P], BF16)
         for G in range(2):
             nc.tensor.transpose(f_ps[:, G, :], f_rows[:, G * P : (G + 1) * P], ident_b[:])
-        warm_up(10)
+        warm_up(12)
 
         hw = [kept("hw%d" % G, [P, 2, 2 * N], U8) for G in range(2)]
         hs = kept("hs", [P, 2, LIGHTS], U8)
@@ -258,8 +258,8 @@ def tile_blinn_phong_radiance_s12_kernel(
                 lobe_mx[c, G] = (kept("l%d%d_codes" % (c, G), [P, N], U32), kept("l%d%d_scales" % (c, G), [P, N], U8))
             cols = slice(h * HALF, (h + 1) * HALF)
             nc.scalar.activation(
-                lobe_bf[c, G][:, cols, :].rearrange("p (c i) t -> p c t i", i=4),
-                relu_t[c, G][:, :, cols].rearrange("p t (c i) -> p c t i", i=4),
+                lobe_bf[c, G][:, cols, :].rearrange("p (c i) t -> p c t i", i=2),
+                relu_t[c, G][:, :, cols].rearrange("p t (c i) -> p c t i", i=2),
                 ACT.Square,
             )
 
@@ -322,17 +322,17 @@ def tile_blinn_phong_radiance_s12_kernel(
         emission_turn(0, 0)
         emission_turn(0, 1)
         lobe_quantize(0, 0)
-        cosines(1, 0, 0, "V")
-        basis_interleave(1)
-        cosines(1, 0, 1, "S")
         emission_turn(1, 0)
-        emission_quantize(0)
         emission_turn(1, 1)
-        cosines(1, 0, 2, "V")
+        basis_interleave(1)
+        cosines(1, 0, 0, "S")
+        emission_quantize(0)
+        cosines(1, 0, 1, "S")
         square(0, 1, 0)
-        basis_quantize(1)
-        cosines(1, 0, 3, "V")
+        cosines(1, 0, 2, "V")
         emission_quantize(1)
+        cosines(1, 0, 3, "V")
+        basis_quantize(1)
         square(0, 1, 1)
 
         groups = [(G, vh) for vh in range(2) for G in range(2)]

from contextlib import ExitStack

import concourse.mybir as mybir
from concourse.masks import make_identity

POINTS, FEATS, LIGHTS, COEFS, BANDS = 2048, 1024, 1024, 512, 1024
FLOPS = 2 * (POINTS * FEATS * LIGHTS + LIGHTS * COEFS * BANDS + POINTS * LIGHTS * BANDS)

F32 = mybir.dt.float32
BF16 = mybir.dt.bfloat16
I32 = mybir.dt.int32
U32 = mybir.dt.uint32
U8 = mybir.dt.uint8
FP8X4 = mybir.dt.float8_e4m3fn_x4
FP4X4 = mybir.dt.float4_e2m1fn_x4
ALU = mybir.AluOpType
ACT = mybir.ActivationFunctionType

P = 128
N = 512
CHUNKS = POINTS // N
HALF = N // 2
HALVES = (slice(0, N), slice(N, 2 * N))
SQRT_FLOOR = 2.0 ** -110


def tile_blinn_phong_radiance_s12_kernel(
    tc, normal_words, normal_scales, half_words, half_scales, falloff, emission, basis, out
):
    nc = tc.nc
    with ExitStack() as ctx:
        keep = ctx.enter_context(tc.tile_pool(name="keep", bufs=1))
        ring = ctx.enter_context(tc.tile_pool(name="ring", bufs=4))
        psum = ctx.enter_context(tc.psum_pool(name="psum", bufs=8))
        ctx.enter_context(tc.manual_schedule())

        def kept(name, shape, dtype):
            return keep.tile(shape, dtype, name=name, align_bytes=64)

        def bank(shape, dtype):
            return psum.tile(shape, dtype, name="bank", tag="bank")

        ident_b = kept("ident_b", [P, P], BF16)
        ident_f = kept("ident_f", [P, P], F32)

        f_rows = kept("f_rows", [P, 2 * P], BF16)
        hs_raw = kept("hs_raw", [P, 2, LIGHTS], U8)
        ns_first = kept("ns_first", [P, 2, N], U8)
        ns_rest = kept("ns_rest", [P, 2, POINTS - N], U8)
        warm_bf = kept("warm_bf", [P, N], BF16)
        nc.gpsimd.memset(f_rows[:].bitcast(I32), 0)
        nc.gpsimd.memset(hs_raw[:].bitcast(I32), 0)
        nc.vector.memset(ns_first[:].bitcast(I32), 0)
        nc.vector.memset(warm_bf[:], 1.0)
        make_identity(nc, ident_b[:])
        make_identity(nc, ident_f[:])
        warm_codes = kept("warm_codes", [P, P], U32)
        warm_scales = kept("warm_scales", [P, P], U8)
        nc.vector.quantize_mx(out=warm_codes[:].bitcast(FP8X4), scales=warm_scales[:], in_=warm_bf[:])
        nc.vector.memset(ns_rest[:].bitcast(I32), 0)
        warm_ps = bank([P, 4, P], F32)

        def warm_up(passes):
            for i in range(passes):
                nc.tensor.matmul_mx(
                    out=warm_ps[:, i % 4, :],
                    lhsT=warm_codes[:].bitcast(FP8X4),
                    lhsT_scale=warm_scales[:],
                    rhs=warm_codes[:].bitcast(FP8X4),
                    rhs_scale=warm_scales[:],
                    start=True,
                    stop=True,
                )

        def load_words(name, src, col0):
            t = kept(name, [P, 2, 2 * N], U8)
            view = src.rearrange("g p n -> p g n")[:, :, 2 * col0 : 2 * (col0 + N)]
            nc.sync.dma_start(out=t[:].bitcast(I32), in_=view.bitcast(I32))
            return t

        def load_scales(plane, src, col0, width):
            for quad in range(4):
                view = src[:, 4 * quad : 4 * quad + 4, col0 : col0 + width].rearrange("g r n -> r g n")
                nc.sync.dma_start(out=plane[32 * quad : 32 * quad + 4].bitcast(I32), in_=view.bitcast(I32))

        hw_raw = [None, None]
        nw = [None] * CHUNKS
        nc.sync.dma_start(
            out=f_rows[0:4, :].rearrange("t (a r) -> t a r", r=8),
            in_=falloff.rearrange("(a t r) -> t a r", t=4, r=8),
        )
        load_scales(hs_raw, half_scales, 0, LIGHTS)
        hw_raw[0] = load_words("hw_raw0", half_words, 0)
        nw[0] = load_words("nw0", normal_words, 0)
        load_scales(ns_first, normal_scales, 0, N)
        hw_raw[1] = load_words("hw_raw1", half_words, N)

        def load_basis(vh):
            t = kept("b_raw%d" % vh, [P, 4, N], BF16)
            nc.sync.dma_start(out=t[:], in_=basis.rearrange("(p t) v -> p t v", t=4)[:, :, vh * N : (vh + 1) * N])
            return t

        def load_emission(G):
            t = kept("e_raw%d" % G, [P, 4 * COEFS], BF16)
            nc.sync.dma_start(out=t[:], in_=emission[G * N : (G + 1) * N, :].rearrange("(p i) c -> p (i c)", i=4))
            return t

        b_raw, e_raw = [None, None], [None, None]
        b_raw[0] = load_basis(0)
        e_raw[0] = load_emission(0)
        e_raw[1] = load_emission(1)
        nw[1] = load_words("nw1", normal_words, N)
        load_scales(ns_rest, normal_scales, N, POINTS - N)
        b_raw[1] = load_basis(1)
        nw[2] = load_words("nw2", normal_words, 2 * N)
        nw[3] = load_words("nw3", normal_words, 3 * N)

        warm_up(10)
        f_ps = bank([P, 2, P], BF16)
        for G in range(2):
            nc.tensor.transpose(f_ps[:, G, :], f_rows[:, G * P : (G + 1) * P], ident_b[:])
        warm_up(12)

        hw = [kept("hw%d" % G, [P, 2, 2 * N], U8) for G in range(2)]
        hs = kept("hs", [P, 2, LIGHTS], U8)

        def sort_half_words(G):
            nc.vector.tensor_copy(
                out=hw[G][:].bitcast(I32).rearrange("p g (t q k) -> p g t q k", t=4, k=4),
                in_=hw_raw[G][:].bitcast(I32).rearrange("p g (q t k) -> p g t q k", t=4, k=4),
            )

        sort_half_words(0)
        nc.vector.tensor_copy(
            out=hs[:].bitcast(I32).rearrange("p g (G t q k) -> p (g G) t q k", G=2, t=4, k=2),
            in_=hs_raw[:].bitcast(I32).rearrange("p g (G q t k) -> p (g G) t q k", G=2, t=4, k=2),
        )

        f_val = f_ps[:, :, 0:4]
        f_neg = kept("f_neg", [P, 2, 4], F32)
        f_abs = kept("f_abs", [P, 2, 4], F32)
        f_low = kept("f_low", [P, 2, 4], F32)
        guess = kept("guess", [P, 2, 4], F32)
        half_nz = kept("half_nz", [P, 2, 4], F32)
        inv = kept("inv", [P, 2, 4], F32)
        term_a = kept("term_a", [P, 2, 4], F32)
        term_b = kept("term_b", [P, 2, 4], F32)
        root = kept("root", [P, 2, 4], F32)
        nc.vector.tensor_scalar(f_neg[:], f_val, -1.0, None, ALU.mult)
        nc.vector.scalar_tensor_tensor(f_low[:], f_val, SQRT_FLOOR, f_neg[:], ALU.max, ALU.max)
        nc.scalar.activation(guess[:], f_low[:], ACT.Sqrt)
        nc.vector.tensor_tensor(f_abs[:], f_val, f_neg[:], ALU.max)
        nc.vector.tensor_scalar(half_nz[:], f_abs[:], 0.0, 0.5, ALU.is_gt, ALU.mult)
        nc.vector.reciprocal(inv[:], guess[:])
        nc.vector.tensor_tensor(term_a[:], guess[:], half_nz[:], ALU.mult)
        nc.vector.scalar_tensor_tensor(term_b[:], f_abs[:], 0.5, inv[:], ALU.mult, ALU.mult)
        nc.vector.tensor_tensor(root[:], term_a[:], term_b[:], ALU.add)

        sign2 = kept("sign2", [P, 2, 4], F32)
        sign = kept("sign", [P, 2, 4], F32)

        def falloff_sign():
            nc.vector.tensor_scalar(sign2[:], f_neg[:], 0.0, 2.0, ALU.is_le, ALU.mult)
            nc.vector.tensor_scalar(sign[:], sign2[:], -1.0, None, ALU.add)

        def quantize(name, src):
            width = src.shape[1] // 4
            codes = kept(name + "_codes", [P, width], U32)
            scales = kept(name + "_scales", [P, width], U8)
            nc.vector.quantize_mx(out=codes[:].bitcast(FP8X4), scales=scales[:], in_=src)
            return codes, scales

        def copy_out(engine, dst, src):
            if engine == "V":
                nc.vector.tensor_copy(out=dst, in_=src)
            else:
                nc.scalar.copy(out=dst, in_=src)

        b_bf = [kept("b_bf%d" % vh, [P, N, 4], BF16) for vh in range(2)]
        b_mx = {}

        def basis_interleave(vh):
            nc.vector.tensor_copy(
                out=b_bf[vh][:].rearrange("p (c i) t -> p c t i", i=4),
                in_=b_raw[vh][:].rearrange("p t (c i) -> p c t i", i=4),
            )

        def basis_quantize(vh):
            b_mx[vh] = quantize("b%d" % vh, b_bf[vh][:].rearrange("p v t -> p (v t)"))

        e_bf = [kept("e_bf%d" % G, [P, 4 * N], BF16) for G in range(2)]
        e_mx = {}

        def emission_turn(G, b):
            ps = bank([P, 4, P], F32)
            words = e_raw[G][:].bitcast(F32)
            for x in range(4):
                i, u = 2 * b + x // 2, x % 2
                nc.tensor.transpose(ps[:, x, :], words[:, 256 * i + u : 256 * (i + 1) : 2], ident_f[:])
            dst = e_bf[G][:].bitcast(F32).rearrange("p (t q h b x) -> p b t q h x", t=4, h=2, b=2, x=4)
            nc.scalar.copy(out=dst[:, b], in_=ps[:].rearrange("p x (q t h) -> p t q h x", t=4, h=2))

        def emission_quantize(G):
            e_mx[G] = quantize("e%d" % G, e_bf[G][:])

        r_bf = {(G, vh): kept("r_bf%d%d" % (G, vh), [P, N, 4], BF16) for G in range(2) for vh in range(2)}
        r_mx = {}

        def radiance(G, vb):
            vh, cols = vb // 4, slice((vb % 4) * P, (vb % 4 + 1) * P)
            ps = bank([P, 4, P], F32)
            for t in range(4):
                ts = slice(t * P, (t + 1) * P)
                nc.tensor.matmul_mx(
                    out=ps[:, t, :],
                    lhsT=e_mx[G][0][:, ts].bitcast(FP8X4),
                    lhsT_scale=e_mx[G][1][:, ts],
                    rhs=b_mx[vh][0][:, cols].bitcast(FP8X4),
                    rhs_scale=b_mx[vh][1][:, cols],
                    start=True,
                    stop=True,
                )
            nc.vector.tensor_tensor(
                r_bf[G, vh][:, cols, :],
                ps[:].rearrange("p t n -> p n t"),
                sign[:, G, :].unsqueeze(1).to_broadcast([P, P, 4]),
                ALU.mult,
            )

        def radiance_quantize(G, vh):
            r_mx[G, vh] = quantize("r%d%d" % (G, vh), r_bf[G, vh][:].rearrange("p v t -> p (v t)"))

        relu_t, lobe_bf, lobe_mx = {}, {}, {}

        def cosines(c, G, t, engine):
            if t == 0:
                relu_t[c, G] = ring.tile([P, 4, N], F32, name="relu_t", tag="relu_t", bufs=5)
            ps = bank([P, N], F32)
            for g in range(2):
                n_scale = ns_first[:, g, :] if c == 0 else ns_rest[:, g, (c - 1) * N : c * N]
                nc.tensor.matmul_mx(
                    out=ps[:],
                    lhsT=hw[G][:, g, 2 * t * P : 2 * (t + 1) * P].bitcast(FP4X4),
                    lhsT_scale=hs[:, g, G * N + t * P : G * N + (t + 1) * P],
                    rhs=nw[c][:, g, :].bitcast(FP4X4),
                    rhs_scale=n_scale,
                    start=(g == 0),
                    stop=(g == 1),
                )
            if engine == "V":
                nc.vector.tensor_scalar(relu_t[c, G][:, t, :], ps[:], root[:, G, t : t + 1], 0.0, ALU.mult, ALU.max)
            else:
                nc.scalar.activation(relu_t[c, G][:, t, :], ps[:], ACT.Relu, scale=root[:, G, t : t + 1])

        def square(c, G, h):
            if h == 0:
                lobe_bf[c, G] = ring.tile([P, N, 4], BF16, name="lobe_bf", tag="lobe_bf", align_bytes=64)
                lobe_mx[c, G] = (kept("l%d%d_codes" % (c, G), [P, N], U32), kept("l%d%d_scales" % (c, G), [P, N], U8))
            cols = slice(h * HALF, (h + 1) * HALF)
            nc.scalar.activation(
                lobe_bf[c, G][:, cols, :].rearrange("p (c i) t -> p c t i", i=2),
                relu_t[c, G][:, :, cols].rearrange("p t (c i) -> p c t i", i=2),
                ACT.Square,
            )

        def lobe_quantize(c, G, cols=slice(0, N)):
            codes, scales = lobe_mx[c, G]
            nc.vector.quantize_mx(
                out=codes[:, cols].bitcast(FP8X4),
                scales=scales[:, cols],
                in_=lobe_bf[c, G][:, cols, :].rearrange("p n t -> p (n t)"),
            )

        def shade_columns(c, pt, bands, dst, engine):
            ps = bank([P, bands.stop - bands.start], F32)
            vh = bands.start // N
            moving = slice(bands.start - vh * N, bands.stop - vh * N)
            cols = slice(pt * P, (pt + 1) * P)
            for G in range(2):
                codes, scales = lobe_mx[c, G]
                nc.tensor.matmul_mx(
                    out=ps[:],
                    lhsT=codes[:, cols].bitcast(FP8X4),
                    lhsT_scale=scales[:, cols],
                    rhs=r_mx[G, vh][0][:, moving].bitcast(FP8X4),
                    rhs_scale=r_mx[G, vh][1][:, moving],
                    start=(G == 0),
                    stop=(G == 1),
                )
            copy_out(engine, dst, ps[:])

        def store(c, pt, bands, res):
            nc.sync.dma_start(out=out[c * N + pt * P : c * N + (pt + 1) * P, bands], in_=res[:, bands])

        def staging():
            return ring.tile([P, BANDS], F32, name="res", tag="res", bufs=6)

        def shade(c, pt, bands, engine):
            res = staging()
            shade_columns(c, pt, bands, res[:, bands], engine)
            store(c, pt, bands, res)

        def shade_rows(c, pt, engines):
            res = staging()
            for vh in range(2):
                shade_columns(c, pt, HALVES[vh], res[:, HALVES[vh]], engines[vh])
            store(c, pt, slice(0, BANDS), res)

        sort_half_words(1)
        falloff_sign()
        basis_interleave(0)
        for t in range(4):
            cosines(0, 0, t, "S")
        cosines(0, 1, 0, "V")
        square(0, 0, 0)
        cosines(0, 1, 1, "V")
        basis_quantize(0)
        square(0, 0, 1)
        cosines(0, 1, 2, "V")
        cosines(0, 1, 3, "V")

        emission_turn(0, 0)
        emission_turn(0, 1)
        lobe_quantize(0, 0)
        emission_turn(1, 0)
        emission_turn(1, 1)
        basis_interleave(1)
        cosines(1, 0, 0, "S")
        emission_quantize(0)
        cosines(1, 0, 1, "S")
        square(0, 1, 0)
        cosines(1, 0, 2, "V")
        emission_quantize(1)
        cosines(1, 0, 3, "V")
        basis_quantize(1)
        square(0, 1, 1)

        groups = [(G, vh) for vh in range(2) for G in range(2)]
        beside = [(1, 1), (2, 0), (2, 1)]
        for k, (G, vh) in enumerate(groups):
            for i in range(4):
                radiance(G, 4 * vh + i)
                if k < len(beside):
                    cosines(beside[k][0], beside[k][1], i, "S")
                else:
                    shade(0, i, HALVES[0], "S")
                if i == 0 and k > 0:
                    radiance_quantize(groups[k - 1][0], groups[k - 1][1])
                if i == 2 and k == 0:
                    lobe_quantize(0, 1)
                if i == 2 and k == 2:
                    lobe_quantize(1, 0)
            square(1, k // 2, k % 2)

        cosines(3, 0, 0, "V")
        radiance_quantize(1, 1)
        cosines(3, 0, 1, "V")
        square(2, 0, 0)
        cosines(3, 0, 2, "V")
        lobe_quantize(1, 1)
        cosines(3, 0, 3, "V")
        square(2, 0, 1)
        for pt in range(4):
            shade(0, pt, HALVES[1], "VS"[pt % 2])
            if pt == 2:
                lobe_quantize(2, 0)
        square(2, 1, 0)

        for pt in range(4):
            shade_rows(1, pt, "VV" if pt == 0 else "VS")
            cosines(3, 1, pt, "V")
            if pt == 0:
                square(2, 1, 1)
            elif pt == 1:
                lobe_quantize(2, 1)
                square(3, 0, 0)
            elif pt == 2:
                square(3, 0, 1)
        lobe_quantize(3, 0)

        res = staging()
        shade_columns(2, 0, HALVES[0], res[:, HALVES[0]], "S")
        square(3, 1, 0)
        shade_columns(2, 0, HALVES[1], res[:, HALVES[1]], "V")
        store(2, 0, slice(0, BANDS), res)
        res = staging()
        shade_columns(2, 1, HALVES[0], res[:, HALVES[0]], "V")
        square(3, 1, 1)
        lobe_quantize(3, 1, slice(0, HALF))
        shade_columns(2, 1, HALVES[1], res[:, HALVES[1]], "V")
        store(2, 1, slice(0, BANDS), res)
        res = staging()
        shade_columns(2, 2, HALVES[0], res[:, HALVES[0]], "V")
        lobe_quantize(3, 1, slice(HALF, N))
        shade_columns(2, 2, HALVES[1], res[:, HALVES[1]], "S")
        store(2, 2, slice(0, BANDS), res)
        shade_rows(2, 3, "VS")
        for pt in range(3):
            shade_rows(3, pt, "VS")
        shade(3, 3, HALVES[0], "V")
        shade(3, 3, slice(N, N + HALF), "S")
        shade(3, 3, slice(N + HALF, BANDS), "V")
